import numpy as np
import ml_dtypes


def mxq(x, axis, fmt="e4m3"):
    dtype, down = {"e4m3": (ml_dtypes.float8_e4m3fn, 7), "e5m2": (ml_dtypes.float8_e5m2, 14)}[fmt]
    v = np.moveaxis(np.asarray(x, np.float32).astype(ml_dtypes.bfloat16).astype(np.float64), axis, -1)
    blocks = v.reshape(v.shape[:-1] + (-1, 32))
    amax = np.abs(blocks).max(-1, keepdims=True)
    byte = np.maximum(np.where(amax > 0, np.frexp(amax)[1] - 1 + 127, 0) - down, 1)
    scale = np.exp2(byte - 127.0)
    codes = (blocks / scale).astype(np.float32).astype(dtype).astype(np.float64)
    return np.moveaxis((codes * scale).reshape(v.shape), -1, axis)


WIDE = False


def mx_kscale(k):
    if not WIDE:
        return np.ones(k)
    levels = np.array([10, -10, 5, -5, 0])
    if k % 512:
        return np.exp2(np.random.permutation(np.resize(levels, k // 32))).repeat(32)
    a = np.empty((k // 512, 16))
    for p in range(k // 512):
        a[p, :8] = np.random.permutation(np.resize(levels, 8))
        for g in range(8):
            far = levels[np.abs(levels - a[p, g]) >= 10]
            a[p, g + 8] = far[np.random.randint(len(far))]
    return np.exp2(a.ravel()).repeat(32)


def f64(x):
    return np.asarray(x).astype(np.float64)


def striped(idx):
    return np.tile(idx.reshape(-1, 16).T, (8, 1)).astype(np.uint16)


def unstriped(offs):
    return offs[:16].T.reshape(-1).astype(np.int64)


E2M1 = np.array([0.0, 0.5, 1.0, 1.5, 2.0, 3.0, 4.0, 6.0, -0.0, -0.5, -1.0, -1.5, -2.0, -3.0, -4.0, -6.0])


def pack_weight(w, fmt):
    k, n = w.shape
    w = f64(np.asarray(w, np.float32).astype(ml_dtypes.bfloat16)).reshape(k // 32, 32, n)
    amax = np.abs(w).max(1)
    if fmt == "e4m3":
        byte = np.frexp(amax)[1] - 1 + 127 - 7
    else:
        mant, ex = np.frexp(amax / 6.0)
        byte = np.where(mant > 0.5, ex, ex - 1) + 127
    byte = np.clip(np.where(amax > 0, byte, 1), 1, 254)
    scaled = (w * np.exp2(127.0 - byte)[:, None, :]).reshape(k, n).astype(np.float32)
    by_word = np.ascontiguousarray(scaled.reshape(k // 512, 128, 4, n).transpose(0, 1, 3, 2))
    if fmt == "e4m3":
        words = by_word.astype(ml_dtypes.float8_e4m3fn).view(np.uint8)
    else:
        c = by_word.astype(ml_dtypes.float4_e2m1fn).view(np.uint8) & 0xF
        words = (c[..., 0::2] | (c[..., 1::2] << 4)).reshape(k // 512, 128, 2 * n)
    return np.ascontiguousarray(words), np.ascontiguousarray(byte.astype(np.uint8).reshape(k // 512, 16, n))


def unpack_weight(words, scales, fmt):
    g, _, n = scales.shape
    words = np.ascontiguousarray(words).reshape(g, 128, n, -1)
    if fmt == "e4m3":
        vals = words.view(ml_dtypes.float8_e4m3fn).astype(np.float64)
    else:
        nib = np.empty((g, 128, n, 4), np.uint8)
        nib[..., 0::2] = words & 0xF
        nib[..., 1::2] = words >> 4
        vals = E2M1[nib]
    vals = vals * np.repeat(np.exp2(scales.astype(np.float64) - 127.0), 8, axis=1)[..., None]
    return vals.transpose(0, 1, 3, 2).reshape(g * 512, n)


def gelu(v):
    return 0.5 * v * (1.0 + np.tanh(np.sqrt(2.0 / np.pi) * (v + 0.044715 * v**3)))


K, T, E, C, H, N = 512, 1536, 4, 256, 512, 128


def by_expert(wq, xq):
    return np.concatenate([wq[e].T @ xq[:, e * C:(e + 1) * C] for e in range(E)], axis=1)


def setup_inputs():
    n = np.random.standard_normal
    s = mx_kscale(K)[:, None]
    u = mx_kscale(H)
    w1 = [pack_weight(m, "e2m1") for m in n((E, K, H)) / np.sqrt(K) / s[None] * u[None, None, :]]
    w2 = [pack_weight(m, "e2m1") for m in n((E, H, N)) / np.sqrt(H) / u[None, :, None]]
    return {
        "xT": (n((K, T)) * s).astype(np.float32),
        "w1_words": np.stack([m[0] for m in w1]),
        "w1_scales": np.stack([m[1] for m in w1]),
        "w2_words": np.stack([m[0] for m in w2]),
        "w2_scales": np.stack([m[1] for m in w2]),
        "gate": np.tile(np.random.uniform(0.2, 1.0, E * C), (N, 1)).astype(np.float32),
        "offs": striped(np.random.permutation(T)[:E * C]),
        "dst": striped(np.random.permutation(T)[:E * C]),
    }


def reference(xT, w1_words, w1_scales, w2_words, w2_scales, gate, offs, dst):
    idx = unstriped(offs)
    w1 = np.stack([unpack_weight(w1_words[e], w1_scales[e], "e2m1") for e in range(E)])
    w2 = np.stack([unpack_weight(w2_words[e], w2_scales[e], "e2m1") for e in range(E)])
    xq = mxq(f64(xT)[:, idx], 0, "e4m3")
    h = gelu(by_expert(w1, xq))
    y = by_expert(w2, mxq(h, 0, "e4m3"))
    out = np.zeros((N, T))
    out[:, unstriped(dst)] = f64(gate) * y
    return out

@@ -1,0 +1,206 @@
+from contextlib import ExitStack
+
+import concourse.mybir as mybir
+
+F32 = mybir.dt.float32
+BF16 = mybir.dt.bfloat16
+I32 = mybir.dt.int32
+U32 = mybir.dt.uint32
+U16 = mybir.dt.uint16
+U8 = mybir.dt.uint8
+FP8X4 = mybir.dt.float8_e4m3fn_x4
+FP4X4 = mybir.dt.float4_e2m1fn_x4
+GELU = mybir.ActivationFunctionType.Gelu_apprx_tanh
+MULT = mybir.AluOpType.mult
+
+P = 128
+K, T, E, C, H, N = 512, 1536, 4, 256, 512, 128
+S = E * C
+FLOPS = 2 * S * (K * H + H * N)
+
+
+def tile_moe_two_mlp_gelu_kernel(tc, xT, w1_words, w1_scales, w2_words, w2_scales, gate, offs, dst, out):
+    nc = tc.nc
+    with ExitStack() as ctx:
+        keep = ctx.enter_context(tc.tile_pool(name="keep", bufs=1))
+        ps_a = ctx.enter_context(tc.psum_pool(name="ps_a", bufs=5))
+        ps_y = ctx.enter_context(tc.psum_pool(name="ps_y", bufs=3))
+
+        offs_t = keep.tile([P, S // 16], U16, name="offs_t")
+        dst_t = keep.tile([P, S // 16], U16, name="dst_t")
+        w1_raw = keep.tile([P, E * 2 * H], U8, name="w1_raw", align_bytes=64)
+        w1_perm = keep.tile([P, E * 2 * H], U8, name="w1_perm", align_bytes=64)
+        s1_raw = keep.tile([P, E, H], U8, name="s1_raw", align_bytes=64)
+        s1_perm = keep.tile([P, E * H], U8, name="s1_perm", align_bytes=64)
+        w2_t = keep.tile([P, E, 2 * N], U8, name="w2_t", align_bytes=64)
+        s2_t = keep.tile([P, E, N], U8, name="s2_t", align_bytes=64)
+        gate_t = keep.tile([P, S], F32, name="gate_t")
+        placed = keep.tile([P, T], F32, name="placed")
+        pairs = [keep.tile([P, T, 2], BF16, name="pairs%d" % h, align_bytes=64) for h in range(2)]
+        grouped = keep.tile([P, S, 4], BF16, name="grouped", align_bytes=64)
+        warm = keep.tile([P, 1], F32, name="warm")
+
+        x_rows = xT.rearrange("(p h j) t -> h p j t", h=2, j=2)
+        chunks = [[(0, 512), (512, 512), (1024, 512)], [(0, 512), (512, 512), (1024, 256), (1280, 256)]]
+        x_raw = {}
+
+        def load_x(h, c):
+            t0, n = chunks[h][c]
+            x_raw[h, c] = keep.tile([P, 2, n], F32, name="x_raw%d_%d" % (h, c))
+            nc.sync.dma_start(out=x_raw[h, c][:], in_=x_rows[h, :, :, t0 : t0 + n])
+
+        nc.gpsimd.memset(s1_raw[:].rearrange("p e i -> p (e i)").bitcast(I32), 0)
+        nc.gpsimd.memset(s2_t[:].rearrange("p e i -> p (e i)").bitcast(I32), 0)
+        nc.gpsimd.memset(warm[:], 0.0)
+        nc.gpsimd.memset(placed[:], 0.0)
+        nc.scalar.activation(out=warm[:], in_=warm[:], func=GELU)
+
+        load_x(0, 0)
+        nc.sync.dma_start(offs_t[:], offs)
+        nc.sync.dma_start(
+            out=w1_raw[:].rearrange("p (e b) -> p e b", e=E).bitcast(I32),
+            in_=w1_words[:, 0].rearrange("e p b -> p e b").bitcast(I32),
+        )
+        for q in range(4):
+            nc.scalar.dma_start(
+                out=s1_raw[32 * q : 32 * q + 4, :, :].bitcast(I32),
+                in_=w1_scales[:, 0, 4 * q : 4 * q + 4, :].rearrange("e q i -> q e i").bitcast(I32),
+            )
+        for h, c in ((0, 1), (0, 2), (1, 0), (1, 1), (1, 2), (1, 3)):
+            load_x(h, c)
+        nc.sync.dma_start(
+            out=w2_t[:].bitcast(I32), in_=w2_words[:, 0].rearrange("e p b -> p e b").bitcast(I32)
+        )
+        for q in range(4):
+            nc.sync.dma_start(
+                out=s2_t[32 * q : 32 * q + 4, :, :].bitcast(I32),
+                in_=w2_scales[:, 0, 4 * q : 4 * q + 4, :].rearrange("e q i -> q e i").bitcast(I32),
+            )
+        nc.sync.dma_start(dst_t[:], dst)
+        nc.sync.dma_start(out=gate_t[:], in_=gate)
+
+        nc.vector.tensor_copy(
+            out=w1_perm[:].bitcast(U16).rearrange("p (e j m) -> p e j m", e=E, j=4),
+            in_=w1_raw[:].bitcast(U16).rearrange("p (e m j) -> p e j m", e=E, j=4),
+        )
+        nc.vector.tensor_copy(
+            out=s1_perm[:].rearrange("p (e j m) -> p e j m", e=E, j=4),
+            in_=s1_raw[:].rearrange("p e (m j) -> p e j m", j=4),
+        )
+
+        def pair(engine_copy, h, c, a, n):
+            t0 = chunks[h][c][0]
+            engine_copy(
+                out=pairs[h][:, t0 + a : t0 + a + n, :],
+                in_=x_raw[h, c][:, :, a : a + n].rearrange("p j t -> p t j"),
+            )
+
+        sc, ve = nc.scalar.copy, nc.vector.tensor_copy
+        slot_words = grouped[:].rearrange("p s j -> p (s j)").bitcast(U32).rearrange("p (s h) -> p s h", h=2)
+
+        def gather(h, s0, n):
+            nc.vector.tensor_copy(
+                out=slot_words[:, s0 : s0 + n, h],
+                in_=pairs[h][:].rearrange("p t j -> p (t j)").bitcast(U32).indirect(offs_t[:, s0 // 16 : (s0 + n) // 16]),
+            )
+
+        pair(sc, 0, 0, 0, 512)
+        pair(sc, 0, 1, 0, 512)
+        pair(sc, 0, 2, 0, 256)
+        pair(ve, 0, 2, 256, 256)
+        gather(0, 0, 512)
+        pair(sc, 1, 0, 0, 512)
+        gather(0, 512, 512)
+        pair(sc, 1, 1, 0, 512)
+        pair(sc, 1, 2, 0, 256)
+        pair(ve, 1, 3, 0, 256)
+
+        x_codes, x_scales, h_raw, h_codes, h_scales, y_gated, y_ps = {}, {}, {}, {}, {}, {}, {}
+
+        def quant_x(e):
+            x_codes[e] = keep.tile([P, C], U32, name="x_codes%d" % e, align_bytes=64)
+            x_scales[e] = keep.tile([P, C], U8, name="x_scales%d" % e, align_bytes=64)
+            nc.vector.quantize_mx(
+                out=x_codes[e][:].bitcast(FP8X4),
+                scales=x_scales[e][:],
+                in_=grouped[:, C * e : C * (e + 1), :].rearrange("p s j -> p (s j)"),
+            )
+
+        def layer1(e):
+            h_raw[e] = keep.tile([P, C, 4], BF16, name="h_raw%d" % e, align_bytes=64)
+            for b in range(2):
+                acc = ps_a.tile([P, 4, 128], F32, name="acc")
+                for j in range(4):
+                    w0 = (e * 4 + j) * 128
+                    nc.tensor.matmul_mx(
+                        out=acc[:, j, :],
+                        lhsT=w1_perm[:, 2 * w0 : 2 * (w0 + 128)].bitcast(FP4X4),
+                        lhsT_scale=s1_perm[:, w0 : w0 + 128],
+                        rhs=x_codes[e][:, 128 * b : 128 * (b + 1)].bitcast(FP8X4),
+                        rhs_scale=x_scales[e][:, 128 * b : 128 * (b + 1)],
+                        start=True,
+                        stop=True,
+                    )
+                nc.scalar.activation(
+                    out=h_raw[e][:, 128 * b : 128 * (b + 1), :],
+                    in_=acc[:].rearrange("p j s -> p s j"),
+                    func=GELU,
+                )
+
+        def quant_h(e):
+            h_codes[e] = keep.tile([P, C], U32, name="h_codes%d" % e, align_bytes=64)
+            h_scales[e] = keep.tile([P, C], U8, name="h_scales%d" % e, align_bytes=64)
+            nc.vector.quantize_mx(
+                out=h_codes[e][:].bitcast(FP8X4),
+                scales=h_scales[e][:],
+                in_=h_raw[e][:].rearrange("p s j -> p (s j)"),
+            )
+
+        def layer2(e):
+            y_ps[e] = ps_y.tile([P, C], F32, name="y_ps")
+            nc.tensor.matmul_mx(
+                out=y_ps[e][:],
+                lhsT=w2_t[:, e, :].bitcast(FP4X4),
+                lhsT_scale=s2_t[:, e, :],
+                rhs=h_codes[e][:].bitcast(FP8X4),
+                rhs_scale=h_scales[e][:],
+                start=True,
+                stop=True,
+            )
+
+        def gate_y(e):
+            y_gated[e] = keep.tile([P, C], F32, name="y_gated%d" % e)
+            nc.vector.tensor_tensor(y_gated[e][:], y_ps[e][:], gate_t[:, C * e : C * (e + 1)], MULT)
+
+        def scatter(e):
+            nc.vector.tensor_copy(placed[:].indirect(dst_t[:, 16 * e : 16 * (e + 1)]), y_gated[e][:])
+
+        gather(1, 0, 256)
+        gather(1, 256, 256)
+        quant_x(0)
+        layer1(0)
+        gather(1, 512, 256)
+        quant_x(1)
+        layer1(1)
+        gather(1, 768, 256)
+        quant_x(2)
+        layer1(2)
+        quant_h(0)
+        layer2(0)
+        quant_x(3)
+        layer1(3)
+        gate_y(0)
+        quant_h(1)
+        layer2(1)
+        scatter(0)
+        gate_y(1)
+        quant_h(2)
+        layer2(2)
+        scatter(1)
+        gate_y(2)
+        quant_h(3)
+        layer2(3)
+        scatter(2)
+        gate_y(3)
+        scatter(3)
+        nc.sync.dma_start(out=out, in_=placed[:])

@@ -23,8 +23,9 @@ def tile_moe_two_mlp_gelu_kernel(tc, xT, w1_words, w1_scales, w2_words, w2_scale
     nc = tc.nc
     with ExitStack() as ctx:
         keep = ctx.enter_context(tc.tile_pool(name="keep", bufs=1))
-        ps_a = ctx.enter_context(tc.psum_pool(name="ps_a", bufs=5))
-        ps_y = ctx.enter_context(tc.psum_pool(name="ps_y", bufs=3))
+        ps_a = ctx.enter_context(tc.psum_pool(name="ps_a", bufs=4))
+        ps_l = ctx.enter_context(tc.psum_pool(name="ps_l", bufs=1))
+        ps_y = ctx.enter_context(tc.psum_pool(name="ps_y", bufs=1))
 
         offs_t = keep.tile([P, S // 16], U16, name="offs_t")
         dst_t = keep.tile([P, S // 16], U16, name="dst_t")
@@ -36,12 +37,48 @@ def tile_moe_two_mlp_gelu_kernel(tc, xT, w1_words, w1_scales, w2_words, w2_scale
         s2_t = keep.tile([P, E, N], U8, name="s2_t", align_bytes=64)
         gate_t = keep.tile([P, S], F32, name="gate_t")
         placed = keep.tile([P, T], F32, name="placed")
-        pairs = [keep.tile([P, T, 2], BF16, name="pairs%d" % h, align_bytes=64) for h in range(2)]
-        grouped = keep.tile([P, S, 4], BF16, name="grouped", align_bytes=64)
         warm = keep.tile([P, 1], F32, name="warm")
 
+        nc.gpsimd.memset(s1_raw[:].rearrange("p e i -> p (e i)").bitcast(I32), 0)
+        nc.vector.memset(warm[:], 0.0)
+        nc.scalar.activation(out=warm[:], in_=warm[:], func=GELU)
+        nc.gpsimd.memset(s2_t[:].rearrange("p e i -> p (e i)").bitcast(I32), 0)
+        nc.gpsimd.memset(placed[:], 0.0)
+
+        def load_w1(e0, e1):
+            nc.sync.dma_start(
+                out=w1_raw[:, 2 * H * e0 : 2 * H * e1].rearrange("p (e b) -> p e b", b=2 * H).bitcast(I32),
+                in_=w1_words[e0:e1, 0].rearrange("e p b -> p e b").bitcast(I32),
+            )
+
+        def load_late():
+            nc.sync.dma_start(
+                out=w2_t[:].bitcast(I32), in_=w2_words[:, 0].rearrange("e p b -> p e b").bitcast(I32)
+            )
+            for q in range(4):
+                nc.sync.dma_start(
+                    out=s2_t[32 * q : 32 * q + 4, :, :].bitcast(I32),
+                    in_=w2_scales[:, 0, 4 * q : 4 * q + 4, :].rearrange("e q i -> q e i").bitcast(I32),
+                )
+            nc.sync.dma_start(dst_t[:], dst)
+            nc.sync.dma_start(out=gate_t[:], in_=gate)
+
+        def permute_words(e0, e1):
+            nc.vector.tensor_copy(
+                out=w1_perm[:, 2 * H * e0 : 2 * H * e1].bitcast(U16).rearrange("p (e j m) -> p e j m", j=4, m=P),
+                in_=w1_raw[:, 2 * H * e0 : 2 * H * e1].bitcast(U16).rearrange("p (e m j) -> p e j m", j=4, m=P),
+            )
+
+        def permute_scales():
+            nc.vector.tensor_copy(
+                out=s1_perm[:].rearrange("p (e j m) -> p e j m", e=E, j=4),
+                in_=s1_raw[:].rearrange("p e (m j) -> p e j m", j=4),
+            )
+
+        pairs = [keep.tile([P, T, 2], BF16, name="pairs%d" % h, align_bytes=64) for h in range(2)]
+        grouped = keep.tile([P, S, 4], BF16, name="grouped", align_bytes=64)
         x_rows = xT.rearrange("(p h j) t -> h p j t", h=2, j=2)
-        chunks = [[(0, 512), (512, 512), (1024, 512)], [(0, 512), (512, 512), (1024, 256), (1280, 256)]]
+        chunks = [[(0, 512), (512, 512), (1024, 512)], [(0, 512), (512, 512), (1024, 512)]]
         x_raw = {}
 
         def load_x(h, c):
@@ -49,73 +86,51 @@ def tile_moe_two_mlp_gelu_kernel(tc, xT, w1_words, w1_scales, w2_words, w2_scale
             x_raw[h, c] = keep.tile([P, 2, n], F32, name="x_raw%d_%d" % (h, c))
             nc.sync.dma_start(out=x_raw[h, c][:], in_=x_rows[h, :, :, t0 : t0 + n])
 
-        nc.gpsimd.memset(s1_raw[:].rearrange("p e i -> p (e i)").bitcast(I32), 0)
-        nc.gpsimd.memset(s2_t[:].rearrange("p e i -> p (e i)").bitcast(I32), 0)
-        nc.gpsimd.memset(warm[:], 0.0)
-        nc.gpsimd.memset(placed[:], 0.0)
-        nc.scalar.activation(out=warm[:], in_=warm[:], func=GELU)
-
         load_x(0, 0)
-        nc.sync.dma_start(offs_t[:], offs)
-        nc.sync.dma_start(
-            out=w1_raw[:].rearrange("p (e b) -> p e b", e=E).bitcast(I32),
-            in_=w1_words[:, 0].rearrange("e p b -> p e b").bitcast(I32),
-        )
         for q in range(4):
-            nc.scalar.dma_start(
+            nc.sync.dma_start(
                 out=s1_raw[32 * q : 32 * q + 4, :, :].bitcast(I32),
                 in_=w1_scales[:, 0, 4 * q : 4 * q + 4, :].rearrange("e q i -> q e i").bitcast(I32),
             )
-        for h, c in ((0, 1), (0, 2), (1, 0), (1, 1), (1, 2), (1, 3)):
+        load_w1(0, 1)
+        nc.sync.dma_start(offs_t[:], offs)
+        for h, c in ((0, 1), (0, 2), (1, 0), (1, 1), (1, 2)):
             load_x(h, c)
-        nc.sync.dma_start(
-            out=w2_t[:].bitcast(I32), in_=w2_words[:, 0].rearrange("e p b -> p e b").bitcast(I32)
-        )
-        for q in range(4):
-            nc.sync.dma_start(
-                out=s2_t[32 * q : 32 * q + 4, :, :].bitcast(I32),
-                in_=w2_scales[:, 0, 4 * q : 4 * q + 4, :].rearrange("e q i -> q e i").bitcast(I32),
-            )
-        nc.sync.dma_start(dst_t[:], dst)
-        nc.sync.dma_start(out=gate_t[:], in_=gate)
-
-        nc.vector.tensor_copy(
-            out=w1_perm[:].bitcast(U16).rearrange("p (e j m) -> p e j m", e=E, j=4),
-            in_=w1_raw[:].bitcast(U16).rearrange("p (e m j) -> p e j m", e=E, j=4),
-        )
-        nc.vector.tensor_copy(
-            out=s1_perm[:].rearrange("p (e j m) -> p e j m", e=E, j=4),
-            in_=s1_raw[:].rearrange("p e (m j) -> p e j m", j=4),
-        )
+        load_w1(1, 4)
+        load_late()
 
         def pair(engine_copy, h, c, a, n):
             t0 = chunks[h][c][0]
             engine_copy(
-                out=pairs[h][:, t0 + a : t0 + a + n, :],
-                in_=x_raw[h, c][:, :, a : a + n].rearrange("p j t -> p t j"),
+                out=pairs[h][:, t0 + a : t0 + a + n, :].rearrange("p (c i) j -> p c j i", i=4),
+                in_=x_raw[h, c][:, :, a : a + n].rearrange("p j (c i) -> p c j i", i=4),
             )
 
         sc, ve = nc.scalar.copy, nc.vector.tensor_copy
         slot_words = grouped[:].rearrange("p s j -> p (s j)").bitcast(U32).rearrange("p (s h) -> p s h", h=2)
 
-        def gather(h, s0, n):
+        def pick(h, s0, n):
             nc.vector.tensor_copy(
                 out=slot_words[:, s0 : s0 + n, h],
                 in_=pairs[h][:].rearrange("p t j -> p (t j)").bitcast(U32).indirect(offs_t[:, s0 // 16 : (s0 + n) // 16]),
             )
 
+        def gather(e):
+            pick(1, C * e, C)
+
+        permute_words(0, 1)
+        permute_scales()
         pair(sc, 0, 0, 0, 512)
         pair(sc, 0, 1, 0, 512)
         pair(sc, 0, 2, 0, 256)
         pair(ve, 0, 2, 256, 256)
-        gather(0, 0, 512)
+        pick(0, 0, 1024)
         pair(sc, 1, 0, 0, 512)
-        gather(0, 512, 512)
         pair(sc, 1, 1, 0, 512)
-        pair(sc, 1, 2, 0, 256)
-        pair(ve, 1, 3, 0, 256)
+        pair(sc, 1, 2, 0, 192)
+        pair(ve, 1, 2, 192, 320)
 
-        x_codes, x_scales, h_raw, h_codes, h_scales, y_gated, y_ps = {}, {}, {}, {}, {}, {}, {}
+        x_codes, x_scales = {}, {}
 
         def quant_x(e):
             x_codes[e] = keep.tile([P, C], U32, name="x_codes%d" % e, align_bytes=64)
@@ -126,10 +141,17 @@ def tile_moe_two_mlp_gelu_kernel(tc, xT, w1_words, w1_scales, w2_words, w2_scale
                 in_=grouped[:, C * e : C * (e + 1), :].rearrange("p s j -> p (s j)"),
             )
 
+        acc_tags = {(3, 1): "h2", (2, 0): "s0", (3, 0): "s1"}
+        y_tags = {0: "s0", 1: "s1", 2: "h2"}
+        h_raw, h_codes, h_scales, y_raw, y_ps = {}, {}, {}, {}, {}
+
         def layer1(e):
             h_raw[e] = keep.tile([P, C, 4], BF16, name="h_raw%d" % e, align_bytes=64)
             for b in range(2):
-                acc = ps_a.tile([P, 4, 128], F32, name="acc")
+                if (e, b) in acc_tags:
+                    acc = ps_l.tile([P, 4, 128], F32, name="acc_%d%d" % (e, b), tag=acc_tags[e, b])
+                else:
+                    acc = ps_a.tile([P, 4, 128], F32, name="acc")
                 for j in range(4):
                     w0 = (e * 4 + j) * 128
                     nc.tensor.matmul_mx(
@@ -156,8 +178,11 @@ def tile_moe_two_mlp_gelu_kernel(tc, xT, w1_words, w1_scales, w2_words, w2_scale
                 in_=h_raw[e][:].rearrange("p s j -> p (s j)"),
             )
 
-        def layer2(e):
-            y_ps[e] = ps_y.tile([P, C], F32, name="y_ps")
+        def layer2(e, gated=False):
+            if e in y_tags:
+                y_ps[e] = ps_l.tile([P, C], F32, name="y_ps%d" % e, tag=y_tags[e])
+            else:
+                y_ps[e] = ps_y.tile([P, C], F32, name="y_ps")
             nc.tensor.matmul_mx(
                 out=y_ps[e][:],
                 lhsT=w2_t[:, e, :].bitcast(FP4X4),
@@ -167,40 +192,48 @@ def tile_moe_two_mlp_gelu_kernel(tc, xT, w1_words, w1_scales, w2_words, w2_scale
                 start=True,
                 stop=True,
             )
+            y_raw[e] = keep.tile([P, C], F32, name="y_raw%d" % e)
+            if gated:
+                nc.vector.tensor_tensor(y_raw[e][:], y_ps[e][:], gate_t[:, C * e : C * (e + 1)], MULT)
+            else:
+                nc.scalar.copy(out=y_raw[e][:], in_=y_ps[e][:])
 
-        def gate_y(e):
-            y_gated[e] = keep.tile([P, C], F32, name="y_gated%d" % e)
-            nc.vector.tensor_tensor(y_gated[e][:], y_ps[e][:], gate_t[:, C * e : C * (e + 1)], MULT)
+        def scatter(e, gated=False):
+            if gated:
+                nc.vector.tensor_copy(placed[:].indirect(dst_t[:, 16 * e : 16 * (e + 1)]), y_raw[e][:])
+                return
+            nc.vector.tensor_tensor(
+                placed[:].indirect(dst_t[:, 16 * e : 16 * (e + 1)]),
+                y_raw[e][:],
+                gate_t[:, C * e : C * (e + 1)],
+                MULT,
+            )
 
-        def scatter(e):
-            nc.vector.tensor_copy(placed[:].indirect(dst_t[:, 16 * e : 16 * (e + 1)]), y_gated[e][:])
-
-        gather(1, 0, 256)
-        gather(1, 256, 256)
+        gather(0)
         quant_x(0)
+        permute_words(1, 2)
         layer1(0)
-        gather(1, 512, 256)
+        gather(1)
         quant_x(1)
-        layer1(1)
-        gather(1, 768, 256)
-        quant_x(2)
-        layer1(2)
         quant_h(0)
         layer2(0)
-        quant_x(3)
-        layer1(3)
-        gate_y(0)
-        quant_h(1)
-        layer2(1)
+        layer1(1)
+        permute_words(2, 3)
+        gather(2)
         scatter(0)
-        gate_y(1)
+        gather(3)
+        quant_x(2)
+        layer1(2)
+        quant_x(3)
+        quant_h(1)
+        permute_words(3, 4)
         quant_h(2)
-        layer2(2)
+        layer2(1)
+        layer1(3)
         scatter(1)
-        gate_y(2)
+        layer2(2)
+        scatter(2)
         quant_h(3)
         layer2(3)
-        scatter(2)
-        gate_y(3)
         scatter(3)
         nc.sync.dma_start(out=out, in_=placed[:])

from contextlib import ExitStack

import concourse.mybir as mybir

F32 = mybir.dt.float32
BF16 = mybir.dt.bfloat16
I32 = mybir.dt.int32
U32 = mybir.dt.uint32
U16 = mybir.dt.uint16
U8 = mybir.dt.uint8
FP8X4 = mybir.dt.float8_e4m3fn_x4
FP4X4 = mybir.dt.float4_e2m1fn_x4
GELU = mybir.ActivationFunctionType.Gelu_apprx_tanh
MULT = mybir.AluOpType.mult

P = 128
K, T, E, C, H, N = 512, 1536, 4, 256, 512, 128
S = E * C
FLOPS = 2 * S * (K * H + H * N)


def tile_moe_two_mlp_gelu_kernel(tc, xT, w1_words, w1_scales, w2_words, w2_scales, gate, offs, dst, out):
    nc = tc.nc
    with ExitStack() as ctx:
        keep = ctx.enter_context(tc.tile_pool(name="keep", bufs=1))
        ps_a = ctx.enter_context(tc.psum_pool(name="ps_a", bufs=4))
        ps_l = ctx.enter_context(tc.psum_pool(name="ps_l", bufs=1))
        ps_y = ctx.enter_context(tc.psum_pool(name="ps_y", bufs=1))

        offs_t = keep.tile([P, S // 16], U16, name="offs_t")
        dst_t = keep.tile([P, S // 16], U16, name="dst_t")
        w1_raw = keep.tile([P, E * 2 * H], U8, name="w1_raw", align_bytes=64)
        w1_perm = keep.tile([P, E * 2 * H], U8, name="w1_perm", align_bytes=64)
        s1_raw = keep.tile([P, E, H], U8, name="s1_raw", align_bytes=64)
        s1_perm = keep.tile([P, E * H], U8, name="s1_perm", align_bytes=64)
        w2_t = keep.tile([P, E, 2 * N], U8, name="w2_t", align_bytes=64)
        s2_t = keep.tile([P, E, N], U8, name="s2_t", align_bytes=64)
        gate_t = keep.tile([P, S], F32, name="gate_t")
        placed = keep.tile([P, T], F32, name="placed")
        warm = keep.tile([P, 1], F32, name="warm")

        nc.gpsimd.memset(s1_raw[:].rearrange("p e i -> p (e i)").bitcast(I32), 0)
        nc.vector.memset(warm[:], 0.0)
        nc.scalar.activation(out=warm[:], in_=warm[:], func=GELU)
        nc.gpsimd.memset(s2_t[:].rearrange("p e i -> p (e i)").bitcast(I32), 0)
        nc.gpsimd.memset(placed[:], 0.0)

        def load_w1(e0, e1):
            nc.sync.dma_start(
                out=w1_raw[:, 2 * H * e0 : 2 * H * e1].rearrange("p (e b) -> p e b", b=2 * H).bitcast(I32),
                in_=w1_words[e0:e1, 0].rearrange("e p b -> p e b").bitcast(I32),
            )

        def load_late():
            nc.sync.dma_start(
                out=w2_t[:].bitcast(I32), in_=w2_words[:, 0].rearrange("e p b -> p e b").bitcast(I32)
            )
            for q in range(4):
                nc.sync.dma_start(
                    out=s2_t[32 * q : 32 * q + 4, :, :].bitcast(I32),
                    in_=w2_scales[:, 0, 4 * q : 4 * q + 4, :].rearrange("e q i -> q e i").bitcast(I32),
                )
            nc.sync.dma_start(dst_t[:], dst)
            nc.sync.dma_start(out=gate_t[:], in_=gate)

        def permute_words(e0, e1):
            nc.vector.tensor_copy(
                out=w1_perm[:, 2 * H * e0 : 2 * H * e1].bitcast(U16).rearrange("p (e j m) -> p e j m", j=4, m=P),
                in_=w1_raw[:, 2 * H * e0 : 2 * H * e1].bitcast(U16).rearrange("p (e m j) -> p e j m", j=4, m=P),
            )

        def permute_scales():
            nc.vector.tensor_copy(
                out=s1_perm[:].rearrange("p (e j m) -> p e j m", e=E, j=4),
                in_=s1_raw[:].rearrange("p e (m j) -> p e j m", j=4),
            )

        pairs = [keep.tile([P, T, 2], BF16, name="pairs%d" % h, align_bytes=64) for h in range(2)]
        grouped = keep.tile([P, S, 4], BF16, name="grouped", align_bytes=64)
        x_rows = xT.rearrange("(p h j) t -> h p j t", h=2, j=2)
        chunks = [[(0, 512), (512, 512), (1024, 512)], [(0, 512), (512, 512), (1024, 512)]]
        x_raw = {}

        def load_x(h, c):
            t0, n = chunks[h][c]
            x_raw[h, c] = keep.tile([P, 2, n], F32, name="x_raw%d_%d" % (h, c))
            nc.sync.dma_start(out=x_raw[h, c][:], in_=x_rows[h, :, :, t0 : t0 + n])

        load_x(0, 0)
        for q in range(4):
            nc.sync.dma_start(
                out=s1_raw[32 * q : 32 * q + 4, :, :].bitcast(I32),
                in_=w1_scales[:, 0, 4 * q : 4 * q + 4, :].rearrange("e q i -> q e i").bitcast(I32),
            )
        load_w1(0, 1)
        nc.sync.dma_start(offs_t[:], offs)
        for h, c in ((0, 1), (0, 2), (1, 0), (1, 1), (1, 2)):
            load_x(h, c)
        load_w1(1, 4)
        load_late()

        def pair(engine_copy, h, c, a, n):
            t0 = chunks[h][c][0]
            engine_copy(
                out=pairs[h][:, t0 + a : t0 + a + n, :].rearrange("p (c i) j -> p c j i", i=4),
                in_=x_raw[h, c][:, :, a : a + n].rearrange("p j (c i) -> p c j i", i=4),
            )

        sc, ve = nc.scalar.copy, nc.vector.tensor_copy
        slot_words = grouped[:].rearrange("p s j -> p (s j)").bitcast(U32).rearrange("p (s h) -> p s h", h=2)

        def pick(h, s0, n):
            nc.vector.tensor_copy(
                out=slot_words[:, s0 : s0 + n, h],
                in_=pairs[h][:].rearrange("p t j -> p (t j)").bitcast(U32).indirect(offs_t[:, s0 // 16 : (s0 + n) // 16]),
            )

        def gather(e):
            pick(1, C * e, C)

        permute_words(0, 1)
        permute_scales()
        pair(sc, 0, 0, 0, 512)
        pair(sc, 0, 1, 0, 512)
        pair(sc, 0, 2, 0, 256)
        pair(ve, 0, 2, 256, 256)
        pick(0, 0, 1024)
        pair(sc, 1, 0, 0, 512)
        pair(sc, 1, 1, 0, 512)
        pair(sc, 1, 2, 0, 192)
        pair(ve, 1, 2, 192, 320)

        x_codes, x_scales = {}, {}

        def quant_x(e):
            x_codes[e] = keep.tile([P, C], U32, name="x_codes%d" % e, align_bytes=64)
            x_scales[e] = keep.tile([P, C], U8, name="x_scales%d" % e, align_bytes=64)
            nc.vector.quantize_mx(
                out=x_codes[e][:].bitcast(FP8X4),
                scales=x_scales[e][:],
                in_=grouped[:, C * e : C * (e + 1), :].rearrange("p s j -> p (s j)"),
            )

        acc_tags = {(3, 1): "h2", (2, 0): "s0", (3, 0): "s1"}
        y_tags = {0: "s0", 1: "s1", 2: "h2"}
        h_raw, h_codes, h_scales, y_raw, y_ps = {}, {}, {}, {}, {}

        def layer1(e):
            h_raw[e] = keep.tile([P, C, 4], BF16, name="h_raw%d" % e, align_bytes=64)
            for b in range(2):
                if (e, b) in acc_tags:
                    acc = ps_l.tile([P, 4, 128], F32, name="acc_%d%d" % (e, b), tag=acc_tags[e, b])
                else:
                    acc = ps_a.tile([P, 4, 128], F32, name="acc")
                for j in range(4):
                    w0 = (e * 4 + j) * 128
                    nc.tensor.matmul_mx(
                        out=acc[:, j, :],
                        lhsT=w1_perm[:, 2 * w0 : 2 * (w0 + 128)].bitcast(FP4X4),
                        lhsT_scale=s1_perm[:, w0 : w0 + 128],
                        rhs=x_codes[e][:, 128 * b : 128 * (b + 1)].bitcast(FP8X4),
                        rhs_scale=x_scales[e][:, 128 * b : 128 * (b + 1)],
                        start=True,
                        stop=True,
                    )
                nc.scalar.activation(
                    out=h_raw[e][:, 128 * b : 128 * (b + 1), :],
                    in_=acc[:].rearrange("p j s -> p s j"),
                    func=GELU,
                )

        def quant_h(e):
            h_codes[e] = keep.tile([P, C], U32, name="h_codes%d" % e, align_bytes=64)
            h_scales[e] = keep.tile([P, C], U8, name="h_scales%d" % e, align_bytes=64)
            nc.vector.quantize_mx(
                out=h_codes[e][:].bitcast(FP8X4),
                scales=h_scales[e][:],
                in_=h_raw[e][:].rearrange("p s j -> p (s j)"),
            )

        def layer2(e, gated=False):
            if e in y_tags:
                y_ps[e] = ps_l.tile([P, C], F32, name="y_ps%d" % e, tag=y_tags[e])
            else:
                y_ps[e] = ps_y.tile([P, C], F32, name="y_ps")
            nc.tensor.matmul_mx(
                out=y_ps[e][:],
                lhsT=w2_t[:, e, :].bitcast(FP4X4),
                lhsT_scale=s2_t[:, e, :],
                rhs=h_codes[e][:].bitcast(FP8X4),
                rhs_scale=h_scales[e][:],
                start=True,
                stop=True,
            )
            y_raw[e] = keep.tile([P, C], F32, name="y_raw%d" % e)
            if gated:
                nc.vector.tensor_tensor(y_raw[e][:], y_ps[e][:], gate_t[:, C * e : C * (e + 1)], MULT)
            else:
                nc.scalar.copy(out=y_raw[e][:], in_=y_ps[e][:])

        def scatter(e, gated=False):
            if gated:
                nc.vector.tensor_copy(placed[:].indirect(dst_t[:, 16 * e : 16 * (e + 1)]), y_raw[e][:])
                return
            nc.vector.tensor_tensor(
                placed[:].indirect(dst_t[:, 16 * e : 16 * (e + 1)]),
                y_raw[e][:],
                gate_t[:, C * e : C * (e + 1)],
                MULT,
            )

        gather(0)
        quant_x(0)
        permute_words(1, 2)
        layer1(0)
        gather(1)
        quant_x(1)
        quant_h(0)
        layer2(0)
        layer1(1)
        permute_words(2, 3)
        gather(2)
        scatter(0)
        gather(3)
        quant_x(2)
        layer1(2)
        quant_x(3)
        quant_h(1)
        permute_words(3, 4)
        quant_h(2)
        layer2(1)
        layer1(3)
        scatter(1)
        layer2(2)
        scatter(2)
        quant_h(3)
        layer2(3)
        scatter(3)
        nc.sync.dma_start(out=out, in_=placed[:])
